import numpy as np
import ml_dtypes


def mxq(x, axis, fmt="e4m3"):
    dtype, down = {"e4m3": (ml_dtypes.float8_e4m3fn, 7), "e5m2": (ml_dtypes.float8_e5m2, 14)}[fmt]
    v = np.moveaxis(np.asarray(x, np.float32).astype(ml_dtypes.bfloat16).astype(np.float64), axis, -1)
    blocks = v.reshape(v.shape[:-1] + (-1, 32))
    amax = np.abs(blocks).max(-1, keepdims=True)
    byte = np.maximum(np.where(amax > 0, np.frexp(amax)[1] - 1 + 127, 0) - down, 1)
    scale = np.exp2(byte - 127.0)
    codes = (blocks / scale).astype(np.float32).astype(dtype).astype(np.float64)
    return np.moveaxis((codes * scale).reshape(v.shape), -1, axis)


WIDE = False


def mx_kscale(k):
    if not WIDE:
        return np.ones(k)
    levels = np.array([10, -10, 5, -5, 0])
    if k % 512:
        return np.exp2(np.random.permutation(np.resize(levels, k // 32))).repeat(32)
    a = np.empty((k // 512, 16))
    for p in range(k // 512):
        a[p, :8] = np.random.permutation(np.resize(levels, 8))
        for g in range(8):
            far = levels[np.abs(levels - a[p, g]) >= 10]
            a[p, g + 8] = far[np.random.randint(len(far))]
    return np.exp2(a.ravel()).repeat(32)


def f64(x):
    return np.asarray(x).astype(np.float64)


def striped(idx):
    return np.tile(idx.reshape(-1, 16).T, (8, 1)).astype(np.uint16)


def unstriped(offs):
    return offs[:16].T.reshape(-1).astype(np.int64)


E2M1 = np.array([0.0, 0.5, 1.0, 1.5, 2.0, 3.0, 4.0, 6.0, -0.0, -0.5, -1.0, -1.5, -2.0, -3.0, -4.0, -6.0])


def pack_weight(w, fmt):
    k, n = w.shape
    w = f64(np.asarray(w, np.float32).astype(ml_dtypes.bfloat16)).reshape(k // 32, 32, n)
    amax = np.abs(w).max(1)
    if fmt == "e4m3":
        byte = np.frexp(amax)[1] - 1 + 127 - 7
    else:
        mant, ex = np.frexp(amax / 6.0)
        byte = np.where(mant > 0.5, ex, ex - 1) + 127
    byte = np.clip(np.where(amax > 0, byte, 1), 1, 254)
    scaled = (w * np.exp2(127.0 - byte)[:, None, :]).reshape(k, n).astype(np.float32)
    by_word = np.ascontiguousarray(scaled.reshape(k // 512, 128, 4, n).transpose(0, 1, 3, 2))
    if fmt == "e4m3":
        words = by_word.astype(ml_dtypes.float8_e4m3fn).view(np.uint8)
    else:
        c = by_word.astype(ml_dtypes.float4_e2m1fn).view(np.uint8) & 0xF
        words = (c[..., 0::2] | (c[..., 1::2] << 4)).reshape(k // 512, 128, 2 * n)
    return np.ascontiguousarray(words), np.ascontiguousarray(byte.astype(np.uint8).reshape(k // 512, 16, n))


def unpack_weight(words, scales, fmt):
    g, _, n = scales.shape
    words = np.ascontiguousarray(words).reshape(g, 128, n, -1)
    if fmt == "e4m3":
        vals = words.view(ml_dtypes.float8_e4m3fn).astype(np.float64)
    else:
        nib = np.empty((g, 128, n, 4), np.uint8)
        nib[..., 0::2] = words & 0xF
        nib[..., 1::2] = words >> 4
        vals = E2M1[nib]
    vals = vals * np.repeat(np.exp2(scales.astype(np.float64) - 127.0), 8, axis=1)[..., None]
    return vals.transpose(0, 1, 3, 2).reshape(g * 512, n)


def gelu(v):
    return 0.5 * v * (1.0 + np.tanh(np.sqrt(2.0 / np.pi) * (v + 0.044715 * v**3)))


K, T, S, H, P, N, P2 = 1536, 4096, 1024, 1024, 512, 768, 256

def setup_inputs():
    n = np.random.standard_normal
    s = mx_kscale(K)[:, None]
    u = mx_kscale(H)[:, None]
    tab_words, tab_scales = pack_weight(n((K, T)) * s, "e4m3")
    w1 = (1.5 * n((K, H)) / np.sqrt(K) / s).astype(np.float32)
    gain = (np.exp(0.3 * n(H)) * u[:, 0]).astype(np.float32)
    w4_words, w4_scales = pack_weight(n((H, N)) / np.sqrt(H) / u, "e2m1")
    bias = (0.7 * n(N)).astype(np.float32)
    return {"tab_words": tab_words, "tab_scales": tab_scales,
            "offs": striped(np.random.permutation(T)[:S]),
            "pos1": striped(np.random.permutation(S)[:P]),
            "pos2": striped(np.random.permutation(S)[:P]),
            "pos3": striped(np.random.permutation(P)[:P2]),
            "pos4": striped(np.random.permutation(P)[:P2]),
            "w1": w1, "gain": gain,
            "w4_words": w4_words, "w4_scales": w4_scales, "bias": bias}

def reference(tab_words, tab_scales, offs, pos1, pos2, pos3, pos4, w1, gain, w4_words, w4_scales, bias):
    v = unpack_weight(tab_words, tab_scales, "e4m3")[:, unstriped(offs)]
    a = mxq(f64(w1), 0, "e4m3").T @ v
    h = 0.5 * a * (1.0 + np.tanh(np.sqrt(2.0 / np.pi) * (a + 0.044715 * a ** 3))) * f64(gain)[:, None]
    z = np.maximum(h[:, unstriped(pos1)], h[:, unstriped(pos2)])
    w4 = unpack_weight(w4_words, w4_scales, "e2m1")
    y = (w4.T @ mxq(z, 0, "e4m3")) + f64(bias)[:, None]
    out = y[:, unstriped(pos3)] * np.tanh(y[:, unstriped(pos4)])
    return out

@@ -1,0 +1,254 @@
+from contextlib import ExitStack
+
+import concourse.mybir as mybir
+
+K, T, S, H, M, N, J = 1536, 4096, 1024, 1024, 512, 768, 256
+FLOPS = 2 * K * H * S + 2 * H * N * M
+
+F32 = mybir.dt.float32
+BF16 = mybir.dt.bfloat16
+I32 = mybir.dt.int32
+U32 = mybir.dt.uint32
+U16 = mybir.dt.uint16
+U8 = mybir.dt.uint8
+FP8X4 = mybir.dt.float8_e4m3fn_x4
+FP4X4 = mybir.dt.float4_e2m1fn_x4
+ACT = mybir.ActivationFunctionType
+ALU = mybir.AluOpType
+
+P = 128
+PACK = 4
+PASS = P * PACK
+BANK = 512
+K_PASSES = K // PASS
+R_PASSES = H // PASS
+S_BANKS = S // BANK
+N_TILES = N // P
+
+
+def tile_list_paddy_inlet_turns_kernel(
+    tc, tab_words, tab_scales, offs, pos1, pos2, pos3, pos4, w1, gain, w4_words, w4_scales, bias, out
+):
+    nc = tc.nc
+    with ExitStack() as ctx:
+        keep = ctx.enter_context(tc.tile_pool(name="keep", bufs=1))
+        work = ctx.enter_context(tc.tile_pool(name="work", bufs=1))
+        psum = ctx.enter_context(tc.psum_pool(name="psum", bufs=1))
+
+        def load_list(name, src):
+            tile = keep.tile(list(src.shape), U16, name=name)
+            nc.sync.dma_start(tile[:], src)
+            return tile
+
+        def load_table(a):
+            tile = keep.tile([P, T], U32, name="tab%d" % a, align_bytes=64)
+            nc.sync.dma_start(tile[:].bitcast(I32), tab_words[a].rearrange("p t i -> p (t i)").bitcast(I32))
+            return tile
+
+        def load_w1(a, b, c0, width):
+            tile = keep.tile([P, PACK, width], F32, name="w1raw%d_%d_%d" % (a, b, c0), align_bytes=64)
+            rows = w1[a * PASS : (a + 1) * PASS, b * PASS + c0 : b * PASS + c0 + width]
+            nc.sync.dma_start(tile[:], rows.rearrange("(p i) c -> p i c", i=PACK))
+            return tile
+
+        tab_sc = keep.tile([P, T], U8, name="tab_sc", align_bytes=64)
+        nc.vector.memset(tab_sc[:].bitcast(I32), 0)
+        w4_sc = keep.tile([P, R_PASSES, N], U8, name="w4_sc", align_bytes=64)
+        nc.gpsimd.memset(w4_sc[:].rearrange("p a n -> p (a n)").bitcast(I32), 0)
+
+        offs_t = load_list("offs_t", offs)
+        tab = []
+        raw = {}
+        half = PASS // 2
+        for a in range(K_PASSES):
+            tab.append(load_table(a))
+            if a == 0:
+                for q in range(4):
+                    nc.sync.dma_start(
+                        tab_sc[32 * q : 32 * q + 4 * K_PASSES, :].bitcast(I32),
+                        tab_scales[:, 4 * q : 4 * q + 4, :].bitcast(I32),
+                    )
+            if a < K_PASSES - 1:
+                raw[a, 0] = load_w1(a, 0, 0, PASS)
+        last_raw = [load_w1(K_PASSES - 1, 0, u * half, half) for u in range(2)]
+        pos1_t = load_list("pos1_t", pos1)
+        pos2_t = load_list("pos2_t", pos2)
+        gain_t = keep.tile([P, R_PASSES, PACK], F32, name="gain_t")
+        nc.sync.dma_start(gain_t[:], gain.rearrange("(b p t) -> p b t", b=R_PASSES, t=PACK))
+        for a in range(K_PASSES):
+            raw[a, 1] = load_w1(a, 1, 0, PASS)
+        w4_w = keep.tile([P, R_PASSES, 2 * N], U8, name="w4_w", align_bytes=64)
+        nc.sync.dma_start(w4_w[:].bitcast(I32), w4_words.rearrange("a p n -> p a n").bitcast(I32))
+        for q in range(4):
+            nc.sync.dma_start(
+                w4_sc[32 * q : 32 * q + 4, :, :].bitcast(I32),
+                w4_scales[:, 4 * q : 4 * q + 4, :].rearrange("a r n -> r a n").bitcast(I32),
+            )
+        pos3_t = load_list("pos3_t", pos3)
+        pos4_t = load_list("pos4_t", pos4)
+        bias_t = keep.tile([P, N_TILES], F32, name="bias_t")
+        with nc.allow_non_contiguous_dma(reason="one bias value per output partition"):
+            nc.sync.dma_start(bias_t[:], bias.rearrange("(c p) -> p c", p=P))
+
+        def round_w1(copy, dst, src, m0, m1):
+            copy(
+                dst[:].rearrange("p (t m i) -> p m i t", t=PACK, i=PACK)[:, m0:m1],
+                src.rearrange("p i (m t) -> p m i t", t=PACK),
+            )
+
+        def mx_tiles(name):
+            codes = keep.tile([P, PASS], U32, name=name + "_codes", align_bytes=64)
+            scales = keep.tile([P, PASS], U8, name=name + "_scales", align_bytes=64)
+            return codes, scales
+
+        def quantize(pair, src, c0, c1):
+            codes, scales = pair
+            nc.vector.quantize_mx(
+                out=codes[:, c0:c1].bitcast(FP8X4), scales=scales[:, c0:c1], in_=src[:, PACK * c0 : PACK * c1]
+            )
+
+        def stage_tile(tag):
+            return work.tile([P, PACK * PASS], BF16, name=tag, tag=tag, align_bytes=64)
+
+        v_words = [keep.tile([P, S], U32, name="v_words%d" % a, align_bytes=64) for a in range(K_PASSES)]
+        v_sc = keep.tile([P, S], U8, name="v_sc", align_bytes=64)
+        w1q = {}
+        for a in range(K_PASSES):
+            for b in range(R_PASSES):
+                w1q[a, b] = mx_tiles("w1q%d_%d" % (a, b))
+
+        def gather_table(a, c0, c1):
+            nc.vector.tensor_copy(v_words[a][:, c0:c1], tab[a][:].indirect(offs_t[:, c0 // 16 : c1 // 16]))
+
+        def bank(i):
+            return psum.tile([P, BANK], F32, name="bank%d" % i, tag="bank%d" % i)
+
+        def first_pass(acc, a, b, t, s, first, last):
+            codes, scales = w1q[a, b]
+            nc.tensor.matmul_mx(
+                out=acc[:],
+                lhsT=codes[:, t * P : (t + 1) * P].bitcast(FP8X4),
+                lhsT_scale=scales[:, t * P : (t + 1) * P],
+                rhs=v_words[a][:, s * BANK : (s + 1) * BANK].bitcast(FP8X4),
+                rhs_scale=v_sc[4 * a : P, s * BANK : (s + 1) * BANK],
+                start=first,
+                stop=last,
+            )
+
+        def features(accs, b, t, gain_on_vector):
+            h = work.tile([P, S], F32, name="h", tag="h", bufs=5)
+            g = gain_t[:, b, t : t + 1]
+            for s in range(S_BANKS):
+                cols = slice(s * BANK, (s + 1) * BANK)
+                nc.scalar.activation(h[:, cols], accs[s][:], ACT.Gelu_apprx_tanh)
+                if gain_on_vector:
+                    nc.vector.tensor_scalar(out=h[:, cols], in0=h[:, cols], scalar1=g, scalar2=None, op0=ALU.mult)
+            if not gain_on_vector:
+                for s in range(S_BANKS):
+                    cols = slice(s * BANK, (s + 1) * BANK)
+                    nc.scalar.activation(h[:, cols], h[:, cols], ACT.Copy, scale=g)
+            return h
+
+        def pick_pairs(h, upper, lower, t):
+            nc.vector.tensor_copy(upper[:, t, :], h[:].indirect(pos1_t[:]))
+            nc.vector.tensor_copy(lower[:, t, :], h[:].indirect(pos2_t[:]))
+
+        def join_pairs(z, upper, lower):
+            nc.vector.tensor_tensor(
+                z[:].rearrange("p (c i t) -> p c t i", i=4, t=PACK),
+                upper[:].rearrange("p t (c i) -> p c t i", i=4),
+                lower[:].rearrange("p t (c i) -> p c t i", i=4),
+                ALU.max,
+            )
+
+        acc0 = [[bank(S_BANKS * t + s) for s in range(S_BANKS)] for t in range(PACK)]
+        for a in range(K_PASSES - 1):
+            gather_table(a, 0, S)
+            if a == 0:
+                nc.vector.tensor_copy(v_sc[:], tab_sc[:].indirect(offs_t[:]))
+            staged = stage_tile("stage%d" % a)
+            round_w1(nc.scalar.copy, staged, raw[a, 0][:], 0, P)
+            quantize(w1q[a, 0], staged, 0, PASS)
+            for t in range(PACK):
+                for s in range(S_BANKS):
+                    first_pass(acc0[t][s], a, 0, t, s, a == 0, False)
+        a = K_PASSES - 1
+        gather_table(a, 0, S)
+        staged = stage_tile("stage2")
+        round_w1(nc.scalar.copy, staged, last_raw[0][:], 0, P // 2)
+        round_w1(nc.vector.tensor_copy, staged, last_raw[1][:], P // 2, P)
+        quantize(w1q[a, 0], staged, 0, P)
+        quantize(w1q[a, 0], staged, P, PASS)
+
+        upper = work.tile([P, PACK, M], F32, name="upper", tag="upper")
+        lower = work.tile([P, PACK, M], F32, name="lower", tag="lower")
+        for t in range(PACK):
+            for s in range(S_BANKS):
+                first_pass(acc0[t][s], a, 0, t, s, False, True)
+            h = features(acc0[t], 0, t, t == 0)
+            pick_pairs(h, upper, lower, t)
+
+        staged1 = [stage_tile("stage%d" % a) for a in range(K_PASSES)]
+        round_w1(nc.vector.tensor_copy, staged1[0], raw[0, 1][:, :, :half], 0, P // 2)
+        round_w1(nc.vector.tensor_copy, staged1[0], raw[0, 1][:, :, half:], P // 2, P)
+        round_w1(nc.scalar.copy, staged1[1], raw[1, 1][:], 0, P)
+        round_w1(nc.scalar.copy, staged1[2], raw[2, 1][:], 0, P)
+        acc1 = [[bank(S_BANKS * t + s) for s in range(S_BANKS)] for t in range(PACK)]
+        for a in range(K_PASSES):
+            quantize(w1q[a, 1], staged1[a], 0, PASS)
+            if a < K_PASSES - 1:
+                for t in range(PACK):
+                    for s in range(S_BANKS):
+                        first_pass(acc1[t][s], a, 1, t, s, a == 0, False)
+
+        zq = [mx_tiles("zq%d" % b) for b in range(R_PASSES)]
+        z = stage_tile("stage2")
+        join_pairs(z, upper, lower)
+        quantize(zq[0], z, 0, M)
+
+        upper = work.tile([P, PACK, M], F32, name="upper", tag="upper")
+        lower = work.tile([P, PACK, M], F32, name="lower", tag="lower")
+        for t in range(PACK):
+            accs = acc1[t]
+            for s in range(S_BANKS):
+                first_pass(accs[s], K_PASSES - 1, 1, t, s, False, True)
+            h = features(accs, 1, t, False)
+            pick_pairs(h, upper, lower, t)
+        z = stage_tile("stage0")
+        join_pairs(z, upper, lower)
+        quantize(zq[1], z, 0, M)
+
+        acc2 = [bank(c) for c in range(N_TILES)]
+        for b in range(R_PASSES):
+            codes, scales = zq[b]
+            for c in range(N_TILES):
+                nc.tensor.matmul_mx(
+                    out=acc2[c][:],
+                    lhsT=w4_w[:, b, 2 * c * P : 2 * (c + 1) * P].bitcast(FP4X4),
+                    lhsT_scale=w4_sc[:, b, c * P : (c + 1) * P],
+                    rhs=codes[:].bitcast(FP8X4),
+                    rhs_scale=scales[:],
+                    start=(b == 0),
+                    stop=(b == R_PASSES - 1),
+                )
+
+        ys = []
+        rivals = []
+
+        def finish(c):
+            res = work.tile([P, J], F32, name="res%d" % c)
+            nc.vector.tensor_tensor(res[:], ys[c][:].indirect(pos3_t[:]), rivals[c][:], ALU.mult)
+            nc.sync.dma_start(out[c * P : (c + 1) * P, :], res[:])
+
+        for c in range(N_TILES):
+            y = work.tile([P, M], F32, name="y%d" % c)
+            nc.scalar.activation(y[:], acc2[c][:], ACT.Identity, bias=bias_t[:, c : c + 1])
+            ys.append(y)
+            picked = work.tile([P, J], F32, name="picked", tag="picked", bufs=2)
+            nc.vector.tensor_copy(picked[:], y[:].indirect(pos4_t[:]))
+            rival = work.tile([P, J], F32, name="rival", tag="rival", bufs=3)
+            nc.scalar.activation(rival[:], picked[:], ACT.Tanh)
+            rivals.append(rival)
+            if c > 0:
+                finish(c - 1)
+        finish(N_TILES - 1)

@@ -57,6 +57,13 @@ def tile_list_paddy_inlet_turns_kernel(
         nc.gpsimd.memset(w4_sc[:].rearrange("p a n -> p (a n)").bitcast(I32), 0)
 
         offs_t = load_list("offs_t", offs)
+        gain_t = keep.tile([P, R_PASSES, PACK], F32, name="gain_t")
+        nc.sync.dma_start(gain_t[:], gain.rearrange("(b p t) -> p b t", b=R_PASSES, t=PACK))
+        gain_rows = keep.tile([P, R_PASSES * PACK, M], F32, name="gain_rows")
+        nc.vector.tensor_copy(
+            gain_rows[:],
+            gain_t[:].rearrange("p b t -> p (b t)").unsqueeze(2).to_broadcast([P, R_PASSES * PACK, M]),
+        )
         tab = []
         raw = {}
         half = PASS // 2
@@ -73,8 +80,6 @@ def tile_list_paddy_inlet_turns_kernel(
         last_raw = [load_w1(K_PASSES - 1, 0, u * half, half) for u in range(2)]
         pos1_t = load_list("pos1_t", pos1)
         pos2_t = load_list("pos2_t", pos2)
-        gain_t = keep.tile([P, R_PASSES, PACK], F32, name="gain_t")
-        nc.sync.dma_start(gain_t[:], gain.rearrange("(b p t) -> p b t", b=R_PASSES, t=PACK))
         for a in range(K_PASSES):
             raw[a, 1] = load_w1(a, 1, 0, PASS)
         w4_w = keep.tile([P, R_PASSES, 2 * N], U8, name="w4_w", align_bytes=64)
@@ -135,23 +140,16 @@ def tile_list_paddy_inlet_turns_kernel(
                 stop=last,
             )
 
-        def features(accs, b, t, gain_on_vector):
+        def features(accs):
             h = work.tile([P, S], F32, name="h", tag="h", bufs=5)
-            g = gain_t[:, b, t : t + 1]
             for s in range(S_BANKS):
-                cols = slice(s * BANK, (s + 1) * BANK)
-                nc.scalar.activation(h[:, cols], accs[s][:], ACT.Gelu_apprx_tanh)
-                if gain_on_vector:
-                    nc.vector.tensor_scalar(out=h[:, cols], in0=h[:, cols], scalar1=g, scalar2=None, op0=ALU.mult)
-            if not gain_on_vector:
-                for s in range(S_BANKS):
-                    cols = slice(s * BANK, (s + 1) * BANK)
-                    nc.scalar.activation(h[:, cols], h[:, cols], ACT.Copy, scale=g)
+                nc.scalar.activation(h[:, s * BANK : (s + 1) * BANK], accs[s][:], ACT.Gelu_apprx_tanh)
             return h
 
-        def pick_pairs(h, upper, lower, t):
-            nc.vector.tensor_copy(upper[:, t, :], h[:].indirect(pos1_t[:]))
-            nc.vector.tensor_copy(lower[:, t, :], h[:].indirect(pos2_t[:]))
+        def pick_pairs(h, upper, lower, b, t):
+            g = gain_rows[:, PACK * b + t, :]
+            nc.vector.tensor_tensor(upper[:, t, :], h[:].indirect(pos1_t[:]), g, ALU.mult)
+            nc.vector.tensor_tensor(lower[:, t, :], h[:].indirect(pos2_t[:]), g, ALU.mult)
 
         def join_pairs(z, upper, lower):
             nc.vector.tensor_tensor(
@@ -185,21 +183,22 @@ def tile_list_paddy_inlet_turns_kernel(
         for t in range(PACK):
             for s in range(S_BANKS):
                 first_pass(acc0[t][s], a, 0, t, s, False, True)
-            h = features(acc0[t], 0, t, t == 0)
-            pick_pairs(h, upper, lower, t)
+            h = features(acc0[t])
+            pick_pairs(h, upper, lower, 0, t)
+            if t == 0:
+                staged = stage_tile("stage0")
+                round_w1(nc.vector.tensor_copy, staged, raw[0, 1][:], 0, P)
+                quantize(w1q[0, 1], staged, 0, PASS)
 
-        staged1 = [stage_tile("stage%d" % a) for a in range(K_PASSES)]
-        round_w1(nc.vector.tensor_copy, staged1[0], raw[0, 1][:, :, :half], 0, P // 2)
-        round_w1(nc.vector.tensor_copy, staged1[0], raw[0, 1][:, :, half:], P // 2, P)
+        staged1 = [None] + [stage_tile("stage%d" % a) for a in range(1, K_PASSES)]
         round_w1(nc.scalar.copy, staged1[1], raw[1, 1][:], 0, P)
         round_w1(nc.scalar.copy, staged1[2], raw[2, 1][:], 0, P)
         acc1 = [[bank(S_BANKS * t + s) for s in range(S_BANKS)] for t in range(PACK)]
-        for a in range(K_PASSES):
+        for t in range(PACK):
+            for s in range(S_BANKS):
+                first_pass(acc1[t][s], 0, 1, t, s, True, False)
+        for a in range(1, K_PASSES):
             quantize(w1q[a, 1], staged1[a], 0, PASS)
-            if a < K_PASSES - 1:
-                for t in range(PACK):
-                    for s in range(S_BANKS):
-                        first_pass(acc1[t][s], a, 1, t, s, a == 0, False)
 
         zq = [mx_tiles("zq%d" % b) for b in range(R_PASSES)]
         z = stage_tile("stage2")
@@ -210,10 +209,11 @@ def tile_list_paddy_inlet_turns_kernel(
         lower = work.tile([P, PACK, M], F32, name="lower", tag="lower")
         for t in range(PACK):
             accs = acc1[t]
-            for s in range(S_BANKS):
-                first_pass(accs[s], K_PASSES - 1, 1, t, s, False, True)
-            h = features(accs, 1, t, False)
-            pick_pairs(h, upper, lower, t)
+            for a in range(1, K_PASSES):
+                for s in range(S_BANKS):
+                    first_pass(accs[s], a, 1, t, s, False, a == K_PASSES - 1)
+            h = features(accs)
+            pick_pairs(h, upper, lower, 1, t)
         z = stage_tile("stage0")
         join_pairs(z, upper, lower)
         quantize(zq[1], z, 0, M)

@@ -24,6 +24,7 @@ K_PASSES = K // PASS
 R_PASSES = H // PASS
 S_BANKS = S // BANK
 N_TILES = N // P
+RUN = 2
 
 
 def tile_list_paddy_inlet_turns_kernel(
@@ -52,32 +53,30 @@ def tile_list_paddy_inlet_turns_kernel(
             return tile
 
         tab_sc = keep.tile([P, T], U8, name="tab_sc", align_bytes=64)
-        nc.vector.memset(tab_sc[:].bitcast(I32), 0)
+        nc.gpsimd.memset(tab_sc[:].bitcast(I32), 0)
         w4_sc = keep.tile([P, R_PASSES, N], U8, name="w4_sc", align_bytes=64)
-        nc.gpsimd.memset(w4_sc[:].rearrange("p a n -> p (a n)").bitcast(I32), 0)
+        nc.vector.memset(w4_sc[:].rearrange("p a n -> p (a n)").bitcast(I32), 0)
 
-        offs_t = load_list("offs_t", offs)
-        gain_t = keep.tile([P, R_PASSES, PACK], F32, name="gain_t")
-        nc.sync.dma_start(gain_t[:], gain.rearrange("(b p t) -> p b t", b=R_PASSES, t=PACK))
-        gain_rows = keep.tile([P, R_PASSES * PACK, M], F32, name="gain_rows")
-        nc.vector.tensor_copy(
-            gain_rows[:],
-            gain_t[:].rearrange("p b t -> p (b t)").unsqueeze(2).to_broadcast([P, R_PASSES * PACK, M]),
-        )
         tab = []
         raw = {}
         half = PASS // 2
         for a in range(K_PASSES):
             tab.append(load_table(a))
             if a == 0:
+                offs_t = load_list("offs_t", offs)
                 for q in range(4):
-                    nc.sync.dma_start(
+                    nc.gpsimd.dma_start(
                         tab_sc[32 * q : 32 * q + 4 * K_PASSES, :].bitcast(I32),
                         tab_scales[:, 4 * q : 4 * q + 4, :].bitcast(I32),
                     )
-            if a < K_PASSES - 1:
-                raw[a, 0] = load_w1(a, 0, 0, PASS)
-        last_raw = [load_w1(K_PASSES - 1, 0, u * half, half) for u in range(2)]
+                gain_t = keep.tile([P, R_PASSES, PACK], F32, name="gain_t")
+                nc.gpsimd.dma_start(gain_t[:], gain.rearrange("(b p t) -> p b t", b=R_PASSES, t=PACK))
+                gain_rows = keep.tile([P, PACK, M], F32, name="gain_rows")
+                nc.scalar.copy(
+                    gain_rows[:],
+                    gain_t[:, 0, :].unsqueeze(2).to_broadcast([P, PACK, M]),
+                )
+            raw[a, 0] = load_w1(a, 0, 0, PASS)
         pos1_t = load_list("pos1_t", pos1)
         pos2_t = load_list("pos2_t", pos2)
         for a in range(K_PASSES):
@@ -95,11 +94,21 @@ def tile_list_paddy_inlet_turns_kernel(
         with nc.allow_non_contiguous_dma(reason="one bias value per output partition"):
             nc.sync.dma_start(bias_t[:], bias.rearrange("(c p) -> p c", p=P))
 
-        def round_w1(copy, dst, src, m0, m1):
+        def round_w1(copy, dst, src, m0, m1, t0=0, t1=PACK):
             copy(
-                dst[:].rearrange("p (t m i) -> p m i t", t=PACK, i=PACK)[:, m0:m1],
-                src.rearrange("p i (m t) -> p m i t", t=PACK),
+                dst[:].rearrange("p (t m i) -> p m i t", t=PACK, i=PACK)[:, m0:m1, :, t0:t1],
+                src.rearrange("p i (m t) -> p m i t", t=PACK)[:, :, :, t0:t1],
             )
+
+        def weight_piece(copy, a, b, u, tag):
+            staged = work.tile([P, PACK * PASS // 2], BF16, name="piece", tag=tag, align_bytes=64)
+            copy(
+                staged[:].rearrange("p (t m i) -> p m i t", t=2, i=PACK),
+                raw[a, b][:].rearrange("p i (m t) -> p m i t", t=PACK)[:, :, :, 2 * u : 2 * u + 2],
+            )
+            codes, scales = w1q[a, b]
+            cols = slice(u * half, (u + 1) * half)
+            nc.vector.quantize_mx(out=codes[:, cols].bitcast(FP8X4), scales=scales[:, cols], in_=staged[:])
 
         def mx_tiles(name):
             codes = keep.tile([P, PASS], U32, name=name + "_codes", align_bytes=64)
@@ -140,24 +149,39 @@ def tile_list_paddy_inlet_turns_kernel(
                 stop=last,
             )
 
-        def features(accs):
-            h = work.tile([P, S], F32, name="h", tag="h", bufs=5)
+        def features(accs, tag):
+            h = work.tile([P, S], F32, name="h", tag=tag, align_bytes=64)
             for s in range(S_BANKS):
                 nc.scalar.activation(h[:, s * BANK : (s + 1) * BANK], accs[s][:], ACT.Gelu_apprx_tanh)
             return h
 
         def pick_pairs(h, upper, lower, b, t):
-            g = gain_rows[:, PACK * b + t, :]
-            nc.vector.tensor_tensor(upper[:, t, :], h[:].indirect(pos1_t[:]), g, ALU.mult)
-            nc.vector.tensor_tensor(lower[:, t, :], h[:].indirect(pos2_t[:]), g, ALU.mult)
+            if b == 0:
+                g = gain_rows[:, t, :]
+                nc.vector.tensor_tensor(upper[:, t, :], h[:].indirect(pos1_t[:]), g, ALU.mult)
+                nc.vector.tensor_tensor(lower[:, t, :], h[:].indirect(pos2_t[:]), g, ALU.mult)
+            else:
+                for s in range(S_BANKS):
+                    cols = slice(s * BANK, (s + 1) * BANK)
+                    nc.scalar.activation(h[:, cols], h[:, cols], ACT.Copy, scale=gain_t[:, b, t : t + 1])
+                nc.vector.tensor_copy(upper[:, t, :], h[:].indirect(pos1_t[:]))
+                nc.vector.tensor_copy(lower[:, t, :], h[:].indirect(pos2_t[:]))
 
-        def join_pairs(z, upper, lower):
+        def join_pairs(tag, upper, lower, u):
+            z = work.tile([P, PACK * M // 2], BF16, name="z", tag=tag, align_bytes=64)
+            cols = slice(u * M // 2, (u + 1) * M // 2)
             nc.vector.tensor_tensor(
-                z[:].rearrange("p (c i t) -> p c t i", i=4, t=PACK),
-                upper[:].rearrange("p t (c i) -> p c t i", i=4),
-                lower[:].rearrange("p t (c i) -> p c t i", i=4),
+                z[:].rearrange("p (c i t) -> p c t i", i=RUN, t=PACK),
+                upper[:, :, cols].rearrange("p t (c i) -> p c t i", i=RUN),
+                lower[:, :, cols].rearrange("p t (c i) -> p c t i", i=RUN),
                 ALU.max,
             )
+            return z
+
+        def quantize_z(pair, z, u):
+            codes, scales = pair
+            cols = slice(u * M // 2, (u + 1) * M // 2)
+            nc.vector.quantize_mx(out=codes[:, cols].bitcast(FP8X4), scales=scales[:, cols], in_=z[:])
 
         acc0 = [[bank(S_BANKS * t + s) for s in range(S_BANKS)] for t in range(PACK)]
         for a in range(K_PASSES - 1):
@@ -172,65 +196,55 @@ def tile_list_paddy_inlet_turns_kernel(
                     first_pass(acc0[t][s], a, 0, t, s, a == 0, False)
         a = K_PASSES - 1
         gather_table(a, 0, S)
-        staged = stage_tile("stage2")
-        round_w1(nc.scalar.copy, staged, last_raw[0][:], 0, P // 2)
-        round_w1(nc.vector.tensor_copy, staged, last_raw[1][:], P // 2, P)
-        quantize(w1q[a, 0], staged, 0, P)
-        quantize(w1q[a, 0], staged, P, PASS)
+        weight_piece(nc.vector.tensor_copy, a, 0, 0, "stage2")
+        weight_piece(nc.vector.tensor_copy, a, 0, 1, "late1")
 
         upper = work.tile([P, PACK, M], F32, name="upper", tag="upper")
         lower = work.tile([P, PACK, M], F32, name="lower", tag="lower")
         for t in range(PACK):
             for s in range(S_BANKS):
                 first_pass(acc0[t][s], a, 0, t, s, False, True)
-            h = features(acc0[t])
+            if t == PACK - 1:
+                weight_piece(nc.scalar.copy, 0, 1, 0, "stage0")
+                weight_piece(nc.scalar.copy, 1, 1, 0, "stage1")
+            h = features(acc0[t], "stage0" if t == 0 else "h%d" % t)
             pick_pairs(h, upper, lower, 0, t)
-            if t == 0:
-                staged = stage_tile("stage0")
-                round_w1(nc.vector.tensor_copy, staged, raw[0, 1][:], 0, P)
-                quantize(w1q[0, 1], staged, 0, PASS)
 
-        staged1 = [None] + [stage_tile("stage%d" % a) for a in range(1, K_PASSES)]
-        round_w1(nc.scalar.copy, staged1[1], raw[1, 1][:], 0, P)
-        round_w1(nc.scalar.copy, staged1[2], raw[2, 1][:], 0, P)
-        acc1 = [[bank(S_BANKS * t + s) for s in range(S_BANKS)] for t in range(PACK)]
-        for t in range(PACK):
-            for s in range(S_BANKS):
-                first_pass(acc1[t][s], 0, 1, t, s, True, False)
-        for a in range(1, K_PASSES):
-            quantize(w1q[a, 1], staged1[a], 0, PASS)
-
+        weight_piece(nc.scalar.copy, 2, 1, 0, "stage2")
         zq = [mx_tiles("zq%d" % b) for b in range(R_PASSES)]
-        z = stage_tile("stage2")
-        join_pairs(z, upper, lower)
-        quantize(zq[0], z, 0, M)
+        zs = [join_pairs("stage%d" % (2 - u), upper, lower, u) for u in range(2)]
+        for u in range(2):
+            quantize_z(zq[0], zs[u], u)
+        for a in range(K_PASSES):
+            weight_piece(nc.scalar.copy, a, 1, 1, "h1" if a == 0 else "late%d" % a)
 
         upper = work.tile([P, PACK, M], F32, name="upper", tag="upper")
         lower = work.tile([P, PACK, M], F32, name="lower", tag="lower")
         for t in range(PACK):
-            accs = acc1[t]
-            for a in range(1, K_PASSES):
-                for s in range(S_BANKS):
-                    first_pass(accs[s], a, 1, t, s, False, a == K_PASSES - 1)
-            h = features(accs)
+            accs = [bank(S_BANKS * t + s) for s in range(S_BANKS)]
+            for s in range(S_BANKS):
+                for a in range(K_PASSES):
+                    first_pass(accs[s], a, 1, t, s, a == 0, a == K_PASSES - 1)
+            h = features(accs, "h%d" % t)
             pick_pairs(h, upper, lower, 1, t)
-        z = stage_tile("stage0")
-        join_pairs(z, upper, lower)
-        quantize(zq[1], z, 0, M)
+        zs = [join_pairs("stage%d" % u, upper, lower, u) for u in range(2)]
+        for u in range(2):
+            quantize_z(zq[1], zs[u], u)
 
         acc2 = [bank(c) for c in range(N_TILES)]
-        for b in range(R_PASSES):
+        for b, pieces in ((0, [(0, M)]), (1, [(0, M // 2), (M // 2, M)])):
             codes, scales = zq[b]
             for c in range(N_TILES):
-                nc.tensor.matmul_mx(
-                    out=acc2[c][:],
-                    lhsT=w4_w[:, b, 2 * c * P : 2 * (c + 1) * P].bitcast(FP4X4),
-                    lhsT_scale=w4_sc[:, b, c * P : (c + 1) * P],
-                    rhs=codes[:].bitcast(FP8X4),
-                    rhs_scale=scales[:],
-                    start=(b == 0),
-                    stop=(b == R_PASSES - 1),
-                )
+                for m0, m1 in pieces:
+                    nc.tensor.matmul_mx(
+                        out=acc2[c][:, m0:m1],
+                        lhsT=w4_w[:, b, 2 * c * P : 2 * (c + 1) * P].bitcast(FP4X4),
+                        lhsT_scale=w4_sc[:, b, c * P : (c + 1) * P],
+                        rhs=codes[:, m0:m1].bitcast(FP8X4),
+                        rhs_scale=scales[:, m0:m1],
+                        start=(b == 0),
+                        stop=(b == R_PASSES - 1 and m1 == M),
+                    )
 
         ys = []
         rivals = []

@@ -19,12 +19,13 @@ ALU = mybir.AluOpType
 P = 128
 PACK = 4
 PASS = P * PACK
+PIECE = 256
 BANK = 512
+QUADRANTS = 4
 K_PASSES = K // PASS
 R_PASSES = H // PASS
 S_BANKS = S // BANK
 N_TILES = N // P
-RUN = 2
 
 
 def tile_list_paddy_inlet_turns_kernel(
@@ -46,9 +47,9 @@ def tile_list_paddy_inlet_turns_kernel(
             nc.sync.dma_start(tile[:].bitcast(I32), tab_words[a].rearrange("p t i -> p (t i)").bitcast(I32))
             return tile
 
-        def load_w1(a, b, c0, width):
-            tile = keep.tile([P, PACK, width], F32, name="w1raw%d_%d_%d" % (a, b, c0), align_bytes=64)
-            rows = w1[a * PASS : (a + 1) * PASS, b * PASS + c0 : b * PASS + c0 + width]
+        def load_w1(a, b):
+            tile = keep.tile([P, PACK, PASS], F32, name="w1raw%d_%d" % (a, b), align_bytes=64)
+            rows = w1[a * PASS : (a + 1) * PASS, b * PASS : (b + 1) * PASS]
             nc.sync.dma_start(tile[:], rows.rearrange("(p i) c -> p i c", i=PACK))
             return tile
 
@@ -57,36 +58,29 @@ def tile_list_paddy_inlet_turns_kernel(
         w4_sc = keep.tile([P, R_PASSES, N], U8, name="w4_sc", align_bytes=64)
         nc.vector.memset(w4_sc[:].rearrange("p a n -> p (a n)").bitcast(I32), 0)
 
-        tab = []
-        raw = {}
-        half = PASS // 2
-        for a in range(K_PASSES):
+        tab = [load_table(0)]
+        offs_t = load_list("offs_t", offs)
+        for quad in range(QUADRANTS):
+            nc.gpsimd.dma_start(
+                tab_sc[32 * quad : 32 * quad + 4 * K_PASSES, :].bitcast(I32),
+                tab_scales[:, 4 * quad : 4 * quad + 4, :].bitcast(I32),
+            )
+        gain_t = keep.tile([P, R_PASSES, PACK], F32, name="gain_t")
+        nc.gpsimd.dma_start(gain_t[:], gain.rearrange("(b p t) -> p b t", b=R_PASSES, t=PACK))
+        raw = {(0, 0): load_w1(0, 0)}
+        for a in range(1, K_PASSES):
             tab.append(load_table(a))
-            if a == 0:
-                offs_t = load_list("offs_t", offs)
-                for q in range(4):
-                    nc.gpsimd.dma_start(
-                        tab_sc[32 * q : 32 * q + 4 * K_PASSES, :].bitcast(I32),
-                        tab_scales[:, 4 * q : 4 * q + 4, :].bitcast(I32),
-                    )
-                gain_t = keep.tile([P, R_PASSES, PACK], F32, name="gain_t")
-                nc.gpsimd.dma_start(gain_t[:], gain.rearrange("(b p t) -> p b t", b=R_PASSES, t=PACK))
-                gain_rows = keep.tile([P, PACK, M], F32, name="gain_rows")
-                nc.scalar.copy(
-                    gain_rows[:],
-                    gain_t[:, 0, :].unsqueeze(2).to_broadcast([P, PACK, M]),
-                )
-            raw[a, 0] = load_w1(a, 0, 0, PASS)
+            raw[a, 0] = load_w1(a, 0)
         pos1_t = load_list("pos1_t", pos1)
         pos2_t = load_list("pos2_t", pos2)
         for a in range(K_PASSES):
-            raw[a, 1] = load_w1(a, 1, 0, PASS)
+            raw[a, 1] = load_w1(a, 1)
         w4_w = keep.tile([P, R_PASSES, 2 * N], U8, name="w4_w", align_bytes=64)
         nc.sync.dma_start(w4_w[:].bitcast(I32), w4_words.rearrange("a p n -> p a n").bitcast(I32))
-        for q in range(4):
+        for quad in range(QUADRANTS):
             nc.sync.dma_start(
-                w4_sc[32 * q : 32 * q + 4, :, :].bitcast(I32),
-                w4_scales[:, 4 * q : 4 * q + 4, :].rearrange("a r n -> r a n").bitcast(I32),
+                w4_sc[32 * quad : 32 * quad + 4, :, :].bitcast(I32),
+                w4_scales[:, 4 * quad : 4 * quad + 4, :].rearrange("a r n -> r a n").bitcast(I32),
             )
         pos3_t = load_list("pos3_t", pos3)
         pos4_t = load_list("pos4_t", pos4)
@@ -94,35 +88,14 @@ def tile_list_paddy_inlet_turns_kernel(
         with nc.allow_non_contiguous_dma(reason="one bias value per output partition"):
             nc.sync.dma_start(bias_t[:], bias.rearrange("(c p) -> p c", p=P))
 
-        def round_w1(copy, dst, src, m0, m1, t0=0, t1=PACK):
-            copy(
-                dst[:].rearrange("p (t m i) -> p m i t", t=PACK, i=PACK)[:, m0:m1, :, t0:t1],
-                src.rearrange("p i (m t) -> p m i t", t=PACK)[:, :, :, t0:t1],
-            )
-
-        def weight_piece(copy, a, b, u, tag):
-            staged = work.tile([P, PACK * PASS // 2], BF16, name="piece", tag=tag, align_bytes=64)
-            copy(
-                staged[:].rearrange("p (t m i) -> p m i t", t=2, i=PACK),
-                raw[a, b][:].rearrange("p i (m t) -> p m i t", t=PACK)[:, :, :, 2 * u : 2 * u + 2],
-            )
-            codes, scales = w1q[a, b]
-            cols = slice(u * half, (u + 1) * half)
-            nc.vector.quantize_mx(out=codes[:, cols].bitcast(FP8X4), scales=scales[:, cols], in_=staged[:])
-
         def mx_tiles(name):
             codes = keep.tile([P, PASS], U32, name=name + "_codes", align_bytes=64)
             scales = keep.tile([P, PASS], U8, name=name + "_scales", align_bytes=64)
             return codes, scales
 
-        def quantize(pair, src, c0, c1):
+        def quantize(pair, c0, c1, rounded):
             codes, scales = pair
-            nc.vector.quantize_mx(
-                out=codes[:, c0:c1].bitcast(FP8X4), scales=scales[:, c0:c1], in_=src[:, PACK * c0 : PACK * c1]
-            )
-
-        def stage_tile(tag):
-            return work.tile([P, PACK * PASS], BF16, name=tag, tag=tag, align_bytes=64)
+            nc.vector.quantize_mx(out=codes[:, c0:c1].bitcast(FP8X4), scales=scales[:, c0:c1], in_=rounded[:])
 
         v_words = [keep.tile([P, S], U32, name="v_words%d" % a, align_bytes=64) for a in range(K_PASSES)]
         v_sc = keep.tile([P, S], U8, name="v_sc", align_bytes=64)
@@ -131,13 +104,18 @@ def tile_list_paddy_inlet_turns_kernel(
             for b in range(R_PASSES):
                 w1q[a, b] = mx_tiles("w1q%d_%d" % (a, b))
 
-        def gather_table(a, c0, c1):
-            nc.vector.tensor_copy(v_words[a][:, c0:c1], tab[a][:].indirect(offs_t[:, c0 // 16 : c1 // 16]))
+        def weights(copy, a, b, t0, t1, tag):
+            rounded = work.tile([P, PACK * P * (t1 - t0)], BF16, name="rounded", tag=tag, align_bytes=64)
+            copy(
+                rounded[:].rearrange("p (t m i) -> p m i t", t=t1 - t0, i=PACK),
+                raw[a, b][:].rearrange("p i (m t) -> p m i t", t=PACK)[:, :, :, t0:t1],
+            )
+            quantize(w1q[a, b], t0 * P, t1 * P, rounded)
 
         def bank(i):
             return psum.tile([P, BANK], F32, name="bank%d" % i, tag="bank%d" % i)
 
-        def first_pass(acc, a, b, t, s, first, last):
+        def first_product(acc, a, b, t, s):
             codes, scales = w1q[a, b]
             nc.tensor.matmul_mx(
                 out=acc[:],
@@ -145,97 +123,86 @@ def tile_list_paddy_inlet_turns_kernel(
                 lhsT_scale=scales[:, t * P : (t + 1) * P],
                 rhs=v_words[a][:, s * BANK : (s + 1) * BANK].bitcast(FP8X4),
                 rhs_scale=v_sc[4 * a : P, s * BANK : (s + 1) * BANK],
-                start=first,
-                stop=last,
+                start=(a == 0),
+                stop=(a == K_PASSES - 1),
             )
 
-        def features(accs, tag):
-            h = work.tile([P, S], F32, name="h", tag=tag, align_bytes=64)
+        def pick_pairs(accs, b, t, tag, upper, lower):
+            act = work.tile([P, S], F32, name="act", tag=tag, align_bytes=64)
             for s in range(S_BANKS):
-                nc.scalar.activation(h[:, s * BANK : (s + 1) * BANK], accs[s][:], ACT.Gelu_apprx_tanh)
-            return h
+                nc.scalar.activation(act[:, s * BANK : (s + 1) * BANK], accs[s][:], ACT.Gelu_apprx_tanh)
+            g = gain_rows[:, PACK * b + t, :]
+            nc.vector.tensor_tensor(upper[:, t, :], act[:].indirect(pos1_t[:]), g, ALU.mult)
+            nc.vector.tensor_tensor(lower[:, t, :], act[:].indirect(pos2_t[:]), g, ALU.mult)
 
-        def pick_pairs(h, upper, lower, b, t):
-            if b == 0:
-                g = gain_rows[:, t, :]
-                nc.vector.tensor_tensor(upper[:, t, :], h[:].indirect(pos1_t[:]), g, ALU.mult)
-                nc.vector.tensor_tensor(lower[:, t, :], h[:].indirect(pos2_t[:]), g, ALU.mult)
-            else:
-                for s in range(S_BANKS):
-                    cols = slice(s * BANK, (s + 1) * BANK)
-                    nc.scalar.activation(h[:, cols], h[:, cols], ACT.Copy, scale=gain_t[:, b, t : t + 1])
-                nc.vector.tensor_copy(upper[:, t, :], h[:].indirect(pos1_t[:]))
-                nc.vector.tensor_copy(lower[:, t, :], h[:].indirect(pos2_t[:]))
-
-        def join_pairs(tag, upper, lower, u):
-            z = work.tile([P, PACK * M // 2], BF16, name="z", tag=tag, align_bytes=64)
-            cols = slice(u * M // 2, (u + 1) * M // 2)
+        def join_pairs(upper, lower, u, tag):
+            z = work.tile([P, PACK * PIECE], BF16, name="z", tag=tag, align_bytes=64)
+            cols = slice(u * PIECE, (u + 1) * PIECE)
             nc.vector.tensor_tensor(
-                z[:].rearrange("p (c i t) -> p c t i", i=RUN, t=PACK),
-                upper[:, :, cols].rearrange("p t (c i) -> p c t i", i=RUN),
-                lower[:, :, cols].rearrange("p t (c i) -> p c t i", i=RUN),
+                z[:].rearrange("p (c i t) -> p c t i", i=2, t=PACK),
+                upper[:, :, cols].rearrange("p t (c i) -> p c t i", i=2),
+                lower[:, :, cols].rearrange("p t (c i) -> p c t i", i=2),
                 ALU.max,
             )
             return z
 
-        def quantize_z(pair, z, u):
-            codes, scales = pair
-            cols = slice(u * M // 2, (u + 1) * M // 2)
-            nc.vector.quantize_mx(out=codes[:, cols].bitcast(FP8X4), scales=scales[:, cols], in_=z[:])
+        def pair_tiles():
+            upper = work.tile([P, PACK, M], F32, name="upper", tag="upper")
+            lower = work.tile([P, PACK, M], F32, name="lower", tag="lower")
+            return upper, lower
 
+        last = K_PASSES - 1
         acc0 = [[bank(S_BANKS * t + s) for s in range(S_BANKS)] for t in range(PACK)]
-        for a in range(K_PASSES - 1):
-            gather_table(a, 0, S)
+        for a in range(last):
+            nc.vector.tensor_copy(v_words[a][:], tab[a][:].indirect(offs_t[:]))
             if a == 0:
                 nc.vector.tensor_copy(v_sc[:], tab_sc[:].indirect(offs_t[:]))
-            staged = stage_tile("stage%d" % a)
-            round_w1(nc.scalar.copy, staged, raw[a, 0][:], 0, P)
-            quantize(w1q[a, 0], staged, 0, PASS)
+            weights(nc.scalar.copy, a, 0, 0, PACK, "stage%d" % a)
             for t in range(PACK):
                 for s in range(S_BANKS):
-                    first_pass(acc0[t][s], a, 0, t, s, a == 0, False)
-        a = K_PASSES - 1
-        gather_table(a, 0, S)
-        weight_piece(nc.vector.tensor_copy, a, 0, 0, "stage2")
-        weight_piece(nc.vector.tensor_copy, a, 0, 1, "late1")
+                    first_product(acc0[t][s], a, 0, t, s)
+        gain_rows = keep.tile([P, R_PASSES * PACK, M], F32, name="gain_rows")
+        nc.vector.tensor_copy(
+            gain_rows[:],
+            gain_t[:].rearrange("p b t -> p (b t)").unsqueeze(2).to_broadcast([P, R_PASSES * PACK, M]),
+        )
+        nc.vector.tensor_copy(v_words[last][:], tab[last][:].indirect(offs_t[:]))
+        weights(nc.vector.tensor_copy, last, 0, 0, 2, "stage2")
+        weights(nc.vector.tensor_copy, last, 0, 2, PACK, "late1")
 
-        upper = work.tile([P, PACK, M], F32, name="upper", tag="upper")
-        lower = work.tile([P, PACK, M], F32, name="lower", tag="lower")
+        upper, lower = pair_tiles()
         for t in range(PACK):
             for s in range(S_BANKS):
-                first_pass(acc0[t][s], a, 0, t, s, False, True)
+                first_product(acc0[t][s], last, 0, t, s)
             if t == PACK - 1:
-                weight_piece(nc.scalar.copy, 0, 1, 0, "stage0")
-                weight_piece(nc.scalar.copy, 1, 1, 0, "stage1")
-            h = features(acc0[t], "stage0" if t == 0 else "h%d" % t)
-            pick_pairs(h, upper, lower, 0, t)
+                weights(nc.scalar.copy, 0, 1, 0, 2, "stage0")
+                weights(nc.scalar.copy, 1, 1, 0, 2, "stage1")
+            pick_pairs(acc0[t], 0, t, "stage0" if t == 0 else "act%d" % t, upper, lower)
+        weights(nc.scalar.copy, last, 1, 0, 2, "stage2")
 
-        weight_piece(nc.scalar.copy, 2, 1, 0, "stage2")
         zq = [mx_tiles("zq%d" % b) for b in range(R_PASSES)]
-        zs = [join_pairs("stage%d" % (2 - u), upper, lower, u) for u in range(2)]
+        zs = [join_pairs(upper, lower, u, "stage%d" % (2 - u)) for u in range(2)]
         for u in range(2):
-            quantize_z(zq[0], zs[u], u)
+            quantize(zq[0], u * PIECE, (u + 1) * PIECE, zs[u])
         for a in range(K_PASSES):
-            weight_piece(nc.scalar.copy, a, 1, 1, "h1" if a == 0 else "late%d" % a)
+            weights(nc.scalar.copy, a, 1, 2, PACK, "act1" if a == 0 else "late%d" % a)
 
-        upper = work.tile([P, PACK, M], F32, name="upper", tag="upper")
-        lower = work.tile([P, PACK, M], F32, name="lower", tag="lower")
+        upper, lower = pair_tiles()
         for t in range(PACK):
             accs = [bank(S_BANKS * t + s) for s in range(S_BANKS)]
             for s in range(S_BANKS):
                 for a in range(K_PASSES):
-                    first_pass(accs[s], a, 1, t, s, a == 0, a == K_PASSES - 1)
-            h = features(accs, "h%d" % t)
-            pick_pairs(h, upper, lower, 1, t)
-        zs = [join_pairs("stage%d" % u, upper, lower, u) for u in range(2)]
+                    first_product(accs[s], a, 1, t, s)
+            pick_pairs(accs, 1, t, "act%d" % t, upper, lower)
+        zs = [join_pairs(upper, lower, u, "stage%d" % u) for u in range(2)]
         for u in range(2):
-            quantize_z(zq[1], zs[u], u)
+            quantize(zq[1], u * PIECE, (u + 1) * PIECE, zs[u])
 
         acc2 = [bank(c) for c in range(N_TILES)]
-        for b, pieces in ((0, [(0, M)]), (1, [(0, M // 2), (M // 2, M)])):
+        for b, spans in ((0, [(0, M)]), (1, [(0, PIECE), (PIECE, M)])):
             codes, scales = zq[b]
             for c in range(N_TILES):
-                for m0, m1 in pieces:
+                for m0, m1 in spans:
                     nc.tensor.matmul_mx(
                         out=acc2[c][:, m0:m1],
                         lhsT=w4_w[:, b, 2 * c * P : 2 * (c + 1) * P].bitcast(FP4X4),

from contextlib import ExitStack

import concourse.mybir as mybir

K, T, S, H, M, N, J = 1536, 4096, 1024, 1024, 512, 768, 256
FLOPS = 2 * K * H * S + 2 * H * N * M

F32 = mybir.dt.float32
BF16 = mybir.dt.bfloat16
I32 = mybir.dt.int32
U32 = mybir.dt.uint32
U16 = mybir.dt.uint16
U8 = mybir.dt.uint8
FP8X4 = mybir.dt.float8_e4m3fn_x4
FP4X4 = mybir.dt.float4_e2m1fn_x4
ACT = mybir.ActivationFunctionType
ALU = mybir.AluOpType

P = 128
PACK = 4
PASS = P * PACK
PIECE = 256
BANK = 512
QUADRANTS = 4
K_PASSES = K // PASS
R_PASSES = H // PASS
S_BANKS = S // BANK
N_TILES = N // P


def tile_list_paddy_inlet_turns_kernel(
    tc, tab_words, tab_scales, offs, pos1, pos2, pos3, pos4, w1, gain, w4_words, w4_scales, bias, out
):
    nc = tc.nc
    with ExitStack() as ctx:
        keep = ctx.enter_context(tc.tile_pool(name="keep", bufs=1))
        work = ctx.enter_context(tc.tile_pool(name="work", bufs=1))
        psum = ctx.enter_context(tc.psum_pool(name="psum", bufs=1))

        def load_list(name, src):
            tile = keep.tile(list(src.shape), U16, name=name)
            nc.sync.dma_start(tile[:], src)
            return tile

        def load_table(a):
            tile = keep.tile([P, T], U32, name="tab%d" % a, align_bytes=64)
            nc.sync.dma_start(tile[:].bitcast(I32), tab_words[a].rearrange("p t i -> p (t i)").bitcast(I32))
            return tile

        def load_w1(a, b):
            tile = keep.tile([P, PACK, PASS], F32, name="w1raw%d_%d" % (a, b), align_bytes=64)
            rows = w1[a * PASS : (a + 1) * PASS, b * PASS : (b + 1) * PASS]
            nc.sync.dma_start(tile[:], rows.rearrange("(p i) c -> p i c", i=PACK))
            return tile

        tab_sc = keep.tile([P, T], U8, name="tab_sc", align_bytes=64)
        nc.gpsimd.memset(tab_sc[:].bitcast(I32), 0)
        w4_sc = keep.tile([P, R_PASSES, N], U8, name="w4_sc", align_bytes=64)
        nc.vector.memset(w4_sc[:].rearrange("p a n -> p (a n)").bitcast(I32), 0)

        tab = [load_table(0)]
        offs_t = load_list("offs_t", offs)
        for quad in range(QUADRANTS):
            nc.gpsimd.dma_start(
                tab_sc[32 * quad : 32 * quad + 4 * K_PASSES, :].bitcast(I32),
                tab_scales[:, 4 * quad : 4 * quad + 4, :].bitcast(I32),
            )
        gain_t = keep.tile([P, R_PASSES, PACK], F32, name="gain_t")
        nc.gpsimd.dma_start(gain_t[:], gain.rearrange("(b p t) -> p b t", b=R_PASSES, t=PACK))
        raw = {(0, 0): load_w1(0, 0)}
        for a in range(1, K_PASSES):
            tab.append(load_table(a))
            raw[a, 0] = load_w1(a, 0)
        pos1_t = load_list("pos1_t", pos1)
        pos2_t = load_list("pos2_t", pos2)
        for a in range(K_PASSES):
            raw[a, 1] = load_w1(a, 1)
        w4_w = keep.tile([P, R_PASSES, 2 * N], U8, name="w4_w", align_bytes=64)
        nc.sync.dma_start(w4_w[:].bitcast(I32), w4_words.rearrange("a p n -> p a n").bitcast(I32))
        for quad in range(QUADRANTS):
            nc.sync.dma_start(
                w4_sc[32 * quad : 32 * quad + 4, :, :].bitcast(I32),
                w4_scales[:, 4 * quad : 4 * quad + 4, :].rearrange("a r n -> r a n").bitcast(I32),
            )
        pos3_t = load_list("pos3_t", pos3)
        pos4_t = load_list("pos4_t", pos4)
        bias_t = keep.tile([P, N_TILES], F32, name="bias_t")
        with nc.allow_non_contiguous_dma(reason="one bias value per output partition"):
            nc.sync.dma_start(bias_t[:], bias.rearrange("(c p) -> p c", p=P))

        def mx_tiles(name):
            codes = keep.tile([P, PASS], U32, name=name + "_codes", align_bytes=64)
            scales = keep.tile([P, PASS], U8, name=name + "_scales", align_bytes=64)
            return codes, scales

        def quantize(pair, c0, c1, rounded):
            codes, scales = pair
            nc.vector.quantize_mx(out=codes[:, c0:c1].bitcast(FP8X4), scales=scales[:, c0:c1], in_=rounded[:])

        v_words = [keep.tile([P, S], U32, name="v_words%d" % a, align_bytes=64) for a in range(K_PASSES)]
        v_sc = keep.tile([P, S], U8, name="v_sc", align_bytes=64)
        w1q = {}
        for a in range(K_PASSES):
            for b in range(R_PASSES):
                w1q[a, b] = mx_tiles("w1q%d_%d" % (a, b))

        def weights(copy, a, b, t0, t1, tag):
            rounded = work.tile([P, PACK * P * (t1 - t0)], BF16, name="rounded", tag=tag, align_bytes=64)
            copy(
                rounded[:].rearrange("p (t m i) -> p m i t", t=t1 - t0, i=PACK),
                raw[a, b][:].rearrange("p i (m t) -> p m i t", t=PACK)[:, :, :, t0:t1],
            )
            quantize(w1q[a, b], t0 * P, t1 * P, rounded)

        def bank(i):
            return psum.tile([P, BANK], F32, name="bank%d" % i, tag="bank%d" % i)

        def first_product(acc, a, b, t, s):
            codes, scales = w1q[a, b]
            nc.tensor.matmul_mx(
                out=acc[:],
                lhsT=codes[:, t * P : (t + 1) * P].bitcast(FP8X4),
                lhsT_scale=scales[:, t * P : (t + 1) * P],
                rhs=v_words[a][:, s * BANK : (s + 1) * BANK].bitcast(FP8X4),
                rhs_scale=v_sc[4 * a : P, s * BANK : (s + 1) * BANK],
                start=(a == 0),
                stop=(a == K_PASSES - 1),
            )

        def pick_pairs(accs, b, t, tag, upper, lower):
            act = work.tile([P, S], F32, name="act", tag=tag, align_bytes=64)
            for s in range(S_BANKS):
                nc.scalar.activation(act[:, s * BANK : (s + 1) * BANK], accs[s][:], ACT.Gelu_apprx_tanh)
            g = gain_rows[:, PACK * b + t, :]
            nc.vector.tensor_tensor(upper[:, t, :], act[:].indirect(pos1_t[:]), g, ALU.mult)
            nc.vector.tensor_tensor(lower[:, t, :], act[:].indirect(pos2_t[:]), g, ALU.mult)

        def join_pairs(upper, lower, u, tag):
            z = work.tile([P, PACK * PIECE], BF16, name="z", tag=tag, align_bytes=64)
            cols = slice(u * PIECE, (u + 1) * PIECE)
            nc.vector.tensor_tensor(
                z[:].rearrange("p (c i t) -> p c t i", i=2, t=PACK),
                upper[:, :, cols].rearrange("p t (c i) -> p c t i", i=2),
                lower[:, :, cols].rearrange("p t (c i) -> p c t i", i=2),
                ALU.max,
            )
            return z

        def pair_tiles():
            upper = work.tile([P, PACK, M], F32, name="upper", tag="upper")
            lower = work.tile([P, PACK, M], F32, name="lower", tag="lower")
            return upper, lower

        last = K_PASSES - 1
        acc0 = [[bank(S_BANKS * t + s) for s in range(S_BANKS)] for t in range(PACK)]
        for a in range(last):
            nc.vector.tensor_copy(v_words[a][:], tab[a][:].indirect(offs_t[:]))
            if a == 0:
                nc.vector.tensor_copy(v_sc[:], tab_sc[:].indirect(offs_t[:]))
            weights(nc.scalar.copy, a, 0, 0, PACK, "stage%d" % a)
            for t in range(PACK):
                for s in range(S_BANKS):
                    first_product(acc0[t][s], a, 0, t, s)
        gain_rows = keep.tile([P, R_PASSES * PACK, M], F32, name="gain_rows")
        nc.vector.tensor_copy(
            gain_rows[:],
            gain_t[:].rearrange("p b t -> p (b t)").unsqueeze(2).to_broadcast([P, R_PASSES * PACK, M]),
        )
        nc.vector.tensor_copy(v_words[last][:], tab[last][:].indirect(offs_t[:]))
        weights(nc.vector.tensor_copy, last, 0, 0, 2, "stage2")
        weights(nc.vector.tensor_copy, last, 0, 2, PACK, "late1")

        upper, lower = pair_tiles()
        for t in range(PACK):
            for s in range(S_BANKS):
                first_product(acc0[t][s], last, 0, t, s)
            if t == PACK - 1:
                weights(nc.scalar.copy, 0, 1, 0, 2, "stage0")
                weights(nc.scalar.copy, 1, 1, 0, 2, "stage1")
            pick_pairs(acc0[t], 0, t, "stage0" if t == 0 else "act%d" % t, upper, lower)
        weights(nc.scalar.copy, last, 1, 0, 2, "stage2")

        zq = [mx_tiles("zq%d" % b) for b in range(R_PASSES)]
        zs = [join_pairs(upper, lower, u, "stage%d" % (2 - u)) for u in range(2)]
        for u in range(2):
            quantize(zq[0], u * PIECE, (u + 1) * PIECE, zs[u])
        for a in range(K_PASSES):
            weights(nc.scalar.copy, a, 1, 2, PACK, "act1" if a == 0 else "late%d" % a)

        upper, lower = pair_tiles()
        for t in range(PACK):
            accs = [bank(S_BANKS * t + s) for s in range(S_BANKS)]
            for s in range(S_BANKS):
                for a in range(K_PASSES):
                    first_product(accs[s], a, 1, t, s)
            pick_pairs(accs, 1, t, "act%d" % t, upper, lower)
        zs = [join_pairs(upper, lower, u, "stage%d" % u) for u in range(2)]
        for u in range(2):
            quantize(zq[1], u * PIECE, (u + 1) * PIECE, zs[u])

        acc2 = [bank(c) for c in range(N_TILES)]
        for b, spans in ((0, [(0, M)]), (1, [(0, PIECE), (PIECE, M)])):
            codes, scales = zq[b]
            for c in range(N_TILES):
                for m0, m1 in spans:
                    nc.tensor.matmul_mx(
                        out=acc2[c][:, m0:m1],
                        lhsT=w4_w[:, b, 2 * c * P : 2 * (c + 1) * P].bitcast(FP4X4),
                        lhsT_scale=w4_sc[:, b, c * P : (c + 1) * P],
                        rhs=codes[:, m0:m1].bitcast(FP8X4),
                        rhs_scale=scales[:, m0:m1],
                        start=(b == 0),
                        stop=(b == R_PASSES - 1 and m1 == M),
                    )

        ys = []
        rivals = []

        def finish(c):
            res = work.tile([P, J], F32, name="res%d" % c)
            nc.vector.tensor_tensor(res[:], ys[c][:].indirect(pos3_t[:]), rivals[c][:], ALU.mult)
            nc.sync.dma_start(out[c * P : (c + 1) * P, :], res[:])

        for c in range(N_TILES):
            y = work.tile([P, M], F32, name="y%d" % c)
            nc.scalar.activation(y[:], acc2[c][:], ACT.Identity, bias=bias_t[:, c : c + 1])
            ys.append(y)
            picked = work.tile([P, J], F32, name="picked", tag="picked", bufs=2)
            nc.vector.tensor_copy(picked[:], y[:].indirect(pos4_t[:]))
            rival = work.tile([P, J], F32, name="rival", tag="rival", bufs=3)
            nc.scalar.activation(rival[:], picked[:], ACT.Tanh)
            rivals.append(rival)
            if c > 0:
                finish(c - 1)
        finish(N_TILES - 1)
